import numpy as np
import ml_dtypes


def mxq(x, axis, fmt="e4m3"):
    dtype, down = {"e4m3": (ml_dtypes.float8_e4m3fn, 7), "e5m2": (ml_dtypes.float8_e5m2, 14)}[fmt]
    v = np.moveaxis(np.asarray(x, np.float32).astype(ml_dtypes.bfloat16).astype(np.float64), axis, -1)
    blocks = v.reshape(v.shape[:-1] + (-1, 32))
    amax = np.abs(blocks).max(-1, keepdims=True)
    byte = np.maximum(np.where(amax > 0, np.frexp(amax)[1] - 1 + 127, 0) - down, 1)
    scale = np.exp2(byte - 127.0)
    codes = (blocks / scale).astype(np.float32).astype(dtype).astype(np.float64)
    return np.moveaxis((codes * scale).reshape(v.shape), -1, axis)


WIDE = False


def mx_kscale(k):
    if not WIDE:
        return np.ones(k)
    levels = np.array([10, -10, 5, -5, 0])
    if k % 512:
        return np.exp2(np.random.permutation(np.resize(levels, k // 32))).repeat(32)
    a = np.empty((k // 512, 16))
    for p in range(k // 512):
        a[p, :8] = np.random.permutation(np.resize(levels, 8))
        for g in range(8):
            far = levels[np.abs(levels - a[p, g]) >= 10]
            a[p, g + 8] = far[np.random.randint(len(far))]
    return np.exp2(a.ravel()).repeat(32)


def f64(x):
    return np.asarray(x).astype(np.float64)


def striped(idx):
    return np.tile(idx.reshape(-1, 16).T, (8, 1)).astype(np.uint16)


def unstriped(offs):
    return offs[:16].T.reshape(-1).astype(np.int64)


def pack_weight(w):
    k, n = w.shape
    w = f64(np.asarray(w, np.float32).astype(ml_dtypes.bfloat16)).reshape(k // 32, 32, n)
    amax = np.abs(w).max(1)
    byte = np.clip(np.where(amax > 0, np.frexp(amax)[1] - 1 + 127 - 7, 1), 1, 254)
    scaled = (w * np.exp2(127.0 - byte)[:, None, :]).reshape(k, n).astype(np.float32)
    words = np.ascontiguousarray(scaled.reshape(k // 512, 128, 4, n).transpose(0, 1, 3, 2)).astype(ml_dtypes.float8_e4m3fn).view(np.uint8)
    return words, np.ascontiguousarray(byte.astype(np.uint8).reshape(k // 512, 16, n))


def unpack_weight(words, scales):
    g, p, n, _ = words.shape
    vals = np.ascontiguousarray(words).view(ml_dtypes.float8_e4m3fn).astype(np.float64) * np.repeat(np.exp2(scales.astype(np.float64) - 127.0), 8, axis=1)[..., None]
    return vals.transpose(0, 1, 3, 2).reshape(g * 512, n)


def relu2(v):
    return np.maximum(v, 0.0) ** 2


K, T, S, N = 2048, 1024, 512, 512


def setup_inputs():
    n = np.random.standard_normal
    s = mx_kscale(K)[:, None]
    words, scales = pack_weight(n((K, N)) / np.sqrt(K) / s)
    return {
        "xT": (n((K, S)) * s).astype(np.float32),
        "w_words": words,
        "w_scales": scales,
        "b": (0.3 * n((N, 1))).astype(np.float32),
        "gate": np.tile(np.random.uniform(0.2, 1.0, S), (N, 1)).astype(np.float32),
        "offs": striped(np.random.permutation(T)[:S]),
    }


def reference(xT, w_words, w_scales, b, gate, offs):
    w = unpack_weight(w_words, w_scales)
    idx = unstriped(offs)
    xq = mxq(f64(xT), 0, "e4m3")
    y = w.T @ xq
    y = relu2(y + f64(b))
    out = np.zeros((N, T))
    out[:, idx] = f64(gate) * y
    return out

@@ -1,0 +1,144 @@
+from contextlib import ExitStack
+
+import concourse.mybir as mybir
+from concourse.masks import make_identity
+
+K, T, S, N = 2048, 1024, 512, 512
+P = 128
+PACK = 4
+K_PASS = P * PACK
+PASSES = K // K_PASS
+BLOCKS = N // P
+W = 256
+CHUNKS = S // W
+SHARE = 96
+RUN = 4
+
+F32 = mybir.dt.float32
+BF16 = mybir.dt.bfloat16
+I32 = mybir.dt.int32
+U32 = mybir.dt.uint32
+U16 = mybir.dt.uint16
+U8 = mybir.dt.uint8
+FP8X4 = mybir.dt.float8_e4m3fn_x4
+
+RELU = mybir.ActivationFunctionType.Relu
+SQUARE = mybir.ActivationFunctionType.Square
+MULT = mybir.AluOpType.mult
+
+FLOPS = 2 * K * S * N
+BYTES = 4 * K * S + K * N + K * N // 32 + 4 * N + 4 * S + 16 * S + 4 * N * T
+
+
+def tile_picked_place_lin_relu2_sub_l_kernel(tc, xT, w_words, w_scales, b, gate, offs, out):
+    nc = tc.nc
+    with ExitStack() as ctx:
+        keep = ctx.enter_context(tc.tile_pool(name="keep", bufs=1))
+        psum = ctx.enter_context(tc.psum_pool(name="psum", bufs=7))
+        psum_once = ctx.enter_context(tc.psum_pool(name="psum_once", bufs=1))
+
+        offsets = keep.tile([P, S // 16], U16, name="offsets")
+        bias = keep.tile([P, BLOCKS], F32, name="bias")
+        bias_rows = keep.tile([P, P], F32, name="bias_rows")
+        identity = keep.tile([P, P], F32, name="identity")
+        gate_first = keep.tile([P, W], F32, name="gate_first")
+        gate_rest = keep.tile([P, S - W], F32, name="gate_rest")
+        w_plane = keep.tile([P, N], U8, align_bytes=64, name="w_plane")
+        w_sizes = (1, 2, 1)
+        w_first = (0, 1, 3)
+        w_codes = [keep.tile([P, PASSES, n * P], U32, align_bytes=64, name=f"w_codes{i}") for i, n in enumerate(w_sizes)]
+        windows = [keep.tile([P, T], F32, name=f"window{m}") for m in range(BLOCKS)]
+        raw = [[keep.tile([P, PACK, W], F32, name=f"raw{c}_{a}") for a in range(PASSES)] for c in range(CHUNKS)]
+        grouped = [keep.tile([P, PASSES, W, PACK], BF16, align_bytes=64, name=f"grouped{c}") for c in range(CHUNKS)]
+        codes = [keep.tile([P, PASSES, W], U32, align_bytes=64, name=f"codes{c}") for c in range(CHUNKS)]
+        plane = [keep.tile([P, PASSES, W], U8, align_bytes=64, name=f"plane{c}") for c in range(CHUNKS)]
+        rect = [keep.tile([P, BLOCKS, W], F32, name=f"rect{c}") for c in range(CHUNKS)]
+        sqr = [keep.tile([P, BLOCKS, W], F32, name=f"sqr{c}") for c in range(CHUNKS)]
+
+        w_rows = w_words.rearrange("a p m r -> p a (m r)")
+
+        def load_x(c):
+            for a in range(PASSES):
+                nc.sync.dma_start(raw[c][a][:], xT[a * K_PASS : (a + 1) * K_PASS, c * W : (c + 1) * W].rearrange("(p j) w -> p j w", j=PACK))
+
+        def load_w(i, a0, a1):
+            m0, n = w_first[i], w_sizes[i]
+            nc.sync.dma_start(w_codes[i][:, a0:a1].bitcast(I32), w_rows[:, a0:a1, m0 * P * 4 : (m0 + n) * P * 4].bitcast(I32))
+
+        nc.gpsimd.memset(bias_rows[:], 0.0)
+        nc.scalar.dma_start(bias_rows[0:BLOCKS, :], b.rearrange("(m p) o -> m (p o)", p=P))
+        nc.gpsimd.memset(w_plane[:].bitcast(U32), 0)
+        for q in range(4):
+            nc.scalar.dma_start(w_plane[32 * q : 32 * q + 16, :].bitcast(I32), w_scales[:, 4 * q : 4 * q + 4, :].bitcast(I32))
+        load_x(0)
+        make_identity(nc, identity[:])
+        turned = psum_once.tile([P, P], F32, name="turned")
+        nc.tensor.transpose(turned[:], bias_rows[:], identity[:])
+        nc.scalar.copy(bias[:], turned[:, 0:BLOCKS])
+        load_w(0, 0, 2)
+        load_w(0, 2, 4)
+        nc.sync.dma_start(gate_first[:], gate[0:P, 0:W])
+        nc.sync.dma_start(offsets[:], offs)
+        load_w(1, 0, 4)
+        load_x(1)
+        load_w(2, 0, 4)
+        nc.sync.dma_start(gate_rest[:], gate[0:P, W:S])
+
+        for m in range(BLOCKS):
+            (nc.vector if m < 2 else nc.gpsimd).memset(windows[m][:], 0.0)
+
+        def interleave(c, a, share):
+            for engine_copy, w0, w1 in ((nc.scalar.copy, 0, share), (nc.vector.tensor_copy, share, W)):
+                if w1 > w0:
+                    engine_copy(
+                        grouped[c][:, a, w0:w1].rearrange("p (g i) j -> p g j i", i=RUN),
+                        raw[c][a][:, :, w0:w1].rearrange("p j (g i) -> p g j i", i=RUN),
+                    )
+
+        def quantize(c, a0, a1):
+            nc.vector.quantize_mx(
+                codes[c][:, a0:a1].rearrange("p a w -> p (a w)").bitcast(FP8X4),
+                plane[c][:, a0:a1].rearrange("p a w -> p (a w)"),
+                grouped[c][:, a0:a1].rearrange("p a w j -> p (a w j)"),
+            )
+
+        def multiply(c, m, e0, e1):
+            i = (m + 1) // 2
+            at = (m - w_first[i]) * P
+            acc = psum.tile([P, e1 - e0], F32, name="acc")
+            for a in range(PASSES):
+                nc.tensor.matmul_mx(
+                    acc[:],
+                    lhsT=w_codes[i][:, a, at : at + P].bitcast(FP8X4),
+                    lhsT_scale=w_plane[4 * a : P, m * P : (m + 1) * P],
+                    rhs=codes[c][:, a, e0:e1].bitcast(FP8X4),
+                    rhs_scale=plane[c][:, a, e0:e1],
+                    start=(a == 0),
+                    stop=(a == PASSES - 1),
+                )
+            nc.scalar.activation(rect[c][:, m, e0:e1], acc[:], RELU, bias=bias[:, m : m + 1])
+            nc.scalar.activation(sqr[c][:, m, e0:e1], rect[c][:, m, e0:e1], SQUARE)
+
+        def scatter(c, m, e0, e1):
+            gates = (gate_first if c == 0 else gate_rest)[:, e0:e1]
+            listed = offsets[:, (c * W + e0) // 16 : (c * W + e1) // 16]
+            nc.vector.tensor_tensor(windows[m][:].indirect(listed), sqr[c][:, m, e0:e1], gates, MULT)
+
+        for a in range(PASSES):
+            interleave(0, a, SHARE)
+            quantize(0, a, a + 1)
+        first = [(0, 0, P), (0, P, W), (1, 0, W), (2, 0, W), (3, 0, W)]
+        for m, e0, e1 in first:
+            multiply(0, m, e0, e1)
+        for m, e0, e1 in first[:-1]:
+            scatter(0, m, e0, e1)
+        for a in range(PASSES):
+            interleave(1, a, W)
+        quantize(1, 0, 2)
+        quantize(1, 2, 4)
+        for m in range(BLOCKS):
+            multiply(1, m, 0, W)
+        scatter(0, 3, 0, W)
+        for m in range(BLOCKS):
+            scatter(1, m, 0, W)
+            nc.sync.dma_start(out[m * P : (m + 1) * P, :], windows[m][:])

@@ -11,7 +11,6 @@ PASSES = K // K_PASS
 BLOCKS = N // P
 W = 256
 CHUNKS = S // W
-SHARE = 96
 RUN = 4
 
 F32 = mybir.dt.float32
@@ -34,78 +33,83 @@ def tile_picked_place_lin_relu2_sub_l_kernel(tc, xT, w_words, w_scales, b, gate,
     nc = tc.nc
     with ExitStack() as ctx:
         keep = ctx.enter_context(tc.tile_pool(name="keep", bufs=1))
-        psum = ctx.enter_context(tc.psum_pool(name="psum", bufs=7))
+        psum = ctx.enter_context(tc.psum_pool(name="psum", bufs=1))
         psum_once = ctx.enter_context(tc.psum_pool(name="psum_once", bufs=1))
+        H = W // 2
 
         offsets = keep.tile([P, S // 16], U16, name="offsets")
         bias = keep.tile([P, BLOCKS], F32, name="bias")
         bias_rows = keep.tile([P, P], F32, name="bias_rows")
         identity = keep.tile([P, P], F32, name="identity")
-        gate_first = keep.tile([P, W], F32, name="gate_first")
-        gate_rest = keep.tile([P, S - W], F32, name="gate_rest")
+        gates = [keep.tile([P, W], F32, name=f"gate{c}") for c in range(CHUNKS)]
         w_plane = keep.tile([P, N], U8, align_bytes=64, name="w_plane")
-        w_sizes = (1, 2, 1)
-        w_first = (0, 1, 3)
+        w_sizes = (1, 1, 2)
+        w_first = (0, 1, 2)
         w_codes = [keep.tile([P, PASSES, n * P], U32, align_bytes=64, name=f"w_codes{i}") for i, n in enumerate(w_sizes)]
-        windows = [keep.tile([P, T], F32, name=f"window{m}") for m in range(BLOCKS)]
-        raw = [[keep.tile([P, PACK, W], F32, name=f"raw{c}_{a}") for a in range(PASSES)] for c in range(CHUNKS)]
-        grouped = [keep.tile([P, PASSES, W, PACK], BF16, align_bytes=64, name=f"grouped{c}") for c in range(CHUNKS)]
+        windows = [keep.tile([P, T], F32, name=f"window{m}") for m in range(BLOCKS - 1)]
+        raw = [
+            [keep.tile([P, PACK, W], F32, name=f"raw{c}_{a}", tag=("late" if (c, a) == (0, 3) else f"raw{c}_{a}")) for a in range(PASSES)]
+            for c in range(CHUNKS)
+        ]
+        grouped = [keep.tile([P, PASSES, W, PACK], BF16, align_bytes=64, name="grouped0")]
         codes = [keep.tile([P, PASSES, W], U32, align_bytes=64, name=f"codes{c}") for c in range(CHUNKS)]
         plane = [keep.tile([P, PASSES, W], U8, align_bytes=64, name=f"plane{c}") for c in range(CHUNKS)]
-        rect = [keep.tile([P, BLOCKS, W], F32, name=f"rect{c}") for c in range(CHUNKS)]
-        sqr = [keep.tile([P, BLOCKS, W], F32, name=f"sqr{c}") for c in range(CHUNKS)]
+        rect_early = keep.tile([P, BLOCKS * W], F32, align_bytes=64, name="rect_early")
+        rect_late = keep.tile([P, BLOCKS * W], F32, name="rect_late")
+        sqr = [keep.tile([P, BLOCKS * W], F32, name=f"sqr{c}") for c in range(CHUNKS)]
 
         w_rows = w_words.rearrange("a p m r -> p a (m r)")
 
-        def load_x(c):
-            for a in range(PASSES):
+        def load_x(c, a0, a1):
+            for a in range(a0, a1):
                 nc.sync.dma_start(raw[c][a][:], xT[a * K_PASS : (a + 1) * K_PASS, c * W : (c + 1) * W].rearrange("(p j) w -> p j w", j=PACK))
 
-        def load_w(i, a0, a1):
+        def load_w(i):
             m0, n = w_first[i], w_sizes[i]
-            nc.sync.dma_start(w_codes[i][:, a0:a1].bitcast(I32), w_rows[:, a0:a1, m0 * P * 4 : (m0 + n) * P * 4].bitcast(I32))
+            nc.sync.dma_start(w_codes[i][:].bitcast(I32), w_rows[:, :, m0 * P * 4 : (m0 + n) * P * 4].bitcast(I32))
 
-        nc.gpsimd.memset(bias_rows[:], 0.0)
-        nc.scalar.dma_start(bias_rows[0:BLOCKS, :], b.rearrange("(m p) o -> m (p o)", p=P))
         nc.gpsimd.memset(w_plane[:].bitcast(U32), 0)
+        load_x(0, 0, 1)
+        nc.sync.dma_start(offsets[:], offs)
+        load_x(0, 1, 2)
         for q in range(4):
-            nc.scalar.dma_start(w_plane[32 * q : 32 * q + 16, :].bitcast(I32), w_scales[:, 4 * q : 4 * q + 4, :].bitcast(I32))
-        load_x(0)
+            nc.sync.dma_start(w_plane[32 * q : 32 * q + 16, :].bitcast(I32), w_scales[:, 4 * q : 4 * q + 4, :].bitcast(I32))
+        nc.gpsimd.memset(bias_rows[:], 0.0)
+        nc.gpsimd.dma_start(bias_rows[0:BLOCKS, :], b.rearrange("(m p) o -> m (p o)", p=P))
+        load_w(0)
+        load_x(0, 2, 4)
         make_identity(nc, identity[:])
         turned = psum_once.tile([P, P], F32, name="turned")
         nc.tensor.transpose(turned[:], bias_rows[:], identity[:])
         nc.scalar.copy(bias[:], turned[:, 0:BLOCKS])
-        load_w(0, 0, 2)
-        load_w(0, 2, 4)
-        nc.sync.dma_start(gate_first[:], gate[0:P, 0:W])
-        nc.sync.dma_start(offsets[:], offs)
-        load_w(1, 0, 4)
-        load_x(1)
-        load_w(2, 0, 4)
-        nc.sync.dma_start(gate_rest[:], gate[0:P, W:S])
+        nc.sync.dma_start(gates[0][:], gate[0:P, 0:W])
+        load_w(1)
+        load_w(2)
+        load_x(1, 0, 4)
+        nc.sync.dma_start(gates[1][:], gate[0:P, W:S])
 
-        for m in range(BLOCKS):
-            (nc.vector if m < 2 else nc.gpsimd).memset(windows[m][:], 0.0)
+        for m in range(BLOCKS - 1):
+            nc.vector.memset(windows[m][:], 0.0)
 
-        def interleave(c, a, share):
-            for engine_copy, w0, w1 in ((nc.scalar.copy, 0, share), (nc.vector.tensor_copy, share, W)):
+        def interleave(c, a, e0, e1, share):
+            for engine_copy, w0, w1 in ((nc.scalar.copy, e0, e0 + share), (nc.vector.tensor_copy, e0 + share, e1)):
                 if w1 > w0:
                     engine_copy(
                         grouped[c][:, a, w0:w1].rearrange("p (g i) j -> p g j i", i=RUN),
                         raw[c][a][:, :, w0:w1].rearrange("p j (g i) -> p g j i", i=RUN),
                     )
 
-        def quantize(c, a0, a1):
+        def quantize(c, a, e0, e1):
             nc.vector.quantize_mx(
-                codes[c][:, a0:a1].rearrange("p a w -> p (a w)").bitcast(FP8X4),
-                plane[c][:, a0:a1].rearrange("p a w -> p (a w)"),
-                grouped[c][:, a0:a1].rearrange("p a w j -> p (a w j)"),
+                codes[c][:, a, e0:e1].bitcast(FP8X4),
+                plane[c][:, a, e0:e1],
+                grouped[c][:, a, e0:e1].rearrange("p w j -> p (w j)"),
             )
 
-        def multiply(c, m, e0, e1):
-            i = (m + 1) // 2
+        def multiply(bank, c, m, e0, e1, rect):
+            i = min(m, 2)
             at = (m - w_first[i]) * P
-            acc = psum.tile([P, e1 - e0], F32, name="acc")
+            acc = psum.tile([P, e1 - e0], F32, name=f"acc{bank}")
             for a in range(PASSES):
                 nc.tensor.matmul_mx(
                     acc[:],
@@ -116,29 +120,39 @@ def tile_picked_place_lin_relu2_sub_l_kernel(tc, xT, w_words, w_scales, b, gate,
                     start=(a == 0),
                     stop=(a == PASSES - 1),
                 )
-            nc.scalar.activation(rect[c][:, m, e0:e1], acc[:], RELU, bias=bias[:, m : m + 1])
-            nc.scalar.activation(sqr[c][:, m, e0:e1], rect[c][:, m, e0:e1], SQUARE)
+            nc.scalar.activation(rect, acc[:], RELU, bias=bias[:, m : m + 1])
 
-        def scatter(c, m, e0, e1):
-            gates = (gate_first if c == 0 else gate_rest)[:, e0:e1]
+        def put_back(c, m, e0, e1, rect, squares):
+            nc.scalar.activation(squares, rect, SQUARE)
             listed = offsets[:, (c * W + e0) // 16 : (c * W + e1) // 16]
-            nc.vector.tensor_tensor(windows[m][:].indirect(listed), sqr[c][:, m, e0:e1], gates, MULT)
+            nc.vector.tensor_tensor(windows[m][:].indirect(listed), squares, gates[c][:, e0:e1], MULT)
 
+        def cell(bank, c, m, e0, e1):
+            rect = (rect_early, rect_late)[c][:, m * W + e0 : m * W + e1]
+            multiply(bank, c, m, e0, e1, rect)
+            put_back(c, m, e0, e1, rect, sqr[c][:, m * W + e0 : m * W + e1])
+
+        for a in range(PASSES - 1):
+            interleave(0, a, 0, W, 96)
+            quantize(0, a, 0, W)
+        for e0 in (0, H):
+            interleave(0, 3, e0, e0 + H, 48)
+            quantize(0, 3, e0, e0 + H)
+        windows.append(keep.tile([P, T], F32, name="window3", tag="late"))
+        nc.vector.memset(windows[3][:], 0.0)
+        for bank, m, e0, e1 in ((0, 0, 0, H), (1, 0, H, W), (2, 1, 0, W), (3, 2, 0, W)):
+            cell(bank, 0, m, e0, e1)
+        multiply(4, 0, 3, 0, W, rect_early[:, 3 * W : 4 * W])
+        grouped.append(keep.tile([P, PASSES, W, PACK], BF16, align_bytes=64, name="grouped1"))
         for a in range(PASSES):
-            interleave(0, a, SHARE)
-            quantize(0, a, a + 1)
-        first = [(0, 0, P), (0, P, W), (1, 0, W), (2, 0, W), (3, 0, W)]
-        for m, e0, e1 in first:
-            multiply(0, m, e0, e1)
-        for m, e0, e1 in first[:-1]:
-            scatter(0, m, e0, e1)
-        for a in range(PASSES):
-            interleave(1, a, W)
-        quantize(1, 0, 2)
-        quantize(1, 2, 4)
-        for m in range(BLOCKS):
-            multiply(1, m, 0, W)
-        scatter(0, 3, 0, W)
-        for m in range(BLOCKS):
-            scatter(1, m, 0, W)
+            interleave(1, a, 0, H, H)
+            interleave(1, a, H, W, H if a < 3 else 64)
+            quantize(1, a, 0, W)
+        put_back(0, 3, 0, W, rect_early[:, 3 * W : 4 * W], raw[1][3][:, 0, :])
+        multiply(0, 1, 0, 0, H, rect_late[:, 0:H])
+        multiply(1, 1, 0, H, W, rect_late[:, H:W])
+        put_back(1, 0, 0, W, rect_late[:, 0:W], sqr[1][:, 0:W])
+        nc.sync.dma_start(out[0:P, :], windows[0][:])
+        for m in range(1, BLOCKS):
+            cell((m - 1) % 2, 1, m, 0, W)
             nc.sync.dma_start(out[m * P : (m + 1) * P, :], windows[m][:])

@@ -11,7 +11,7 @@ PASSES = K // K_PASS
 BLOCKS = N // P
 W = 256
 CHUNKS = S // W
-RUN = 4
+RUN = 2
 
 F32 = mybir.dt.float32
 BF16 = mybir.dt.bfloat16
@@ -146,7 +146,7 @@ def tile_picked_place_lin_relu2_sub_l_kernel(tc, xT, w_words, w_scales, b, gate,
         grouped.append(keep.tile([P, PASSES, W, PACK], BF16, align_bytes=64, name="grouped1"))
         for a in range(PASSES):
             interleave(1, a, 0, H, H)
-            interleave(1, a, H, W, H if a < 3 else 64)
+            interleave(1, a, H, W, H if a < 3 else 0)
             quantize(1, a, 0, W)
         put_back(0, 3, 0, W, rect_early[:, 3 * W : 4 * W], raw[1][3][:, 0, :])
         multiply(0, 1, 0, 0, H, rect_late[:, 0:H])

@@ -24,6 +24,7 @@ FP8X4 = mybir.dt.float8_e4m3fn_x4
 RELU = mybir.ActivationFunctionType.Relu
 SQUARE = mybir.ActivationFunctionType.Square
 MULT = mybir.AluOpType.mult
+ADD = mybir.AluOpType.add
 
 FLOPS = 2 * K * S * N
 BYTES = 4 * K * S + K * N + K * N // 32 + 4 * N + 4 * S + 16 * S + 4 * N * T
@@ -48,7 +49,7 @@ def tile_picked_place_lin_relu2_sub_l_kernel(tc, xT, w_words, w_scales, b, gate,
         w_codes = [keep.tile([P, PASSES, n * P], U32, align_bytes=64, name=f"w_codes{i}") for i, n in enumerate(w_sizes)]
         windows = [keep.tile([P, T], F32, name=f"window{m}") for m in range(BLOCKS - 1)]
         raw = [
-            [keep.tile([P, PACK, W], F32, name=f"raw{c}_{a}", tag=("late" if (c, a) == (0, 3) else f"raw{c}_{a}")) for a in range(PASSES)]
+            [keep.tile([P, PACK, W], F32, name=f"raw{c}_{a}", tag=f"raw{c}_{a}") for a in range(PASSES)]
             for c in range(CHUNKS)
         ]
         grouped = [keep.tile([P, PASSES, W, PACK], BF16, align_bytes=64, name="grouped0")]
@@ -84,8 +85,9 @@ def tile_picked_place_lin_relu2_sub_l_kernel(tc, xT, w_words, w_scales, b, gate,
         nc.scalar.copy(bias[:], turned[:, 0:BLOCKS])
         nc.sync.dma_start(gates[0][:], gate[0:P, 0:W])
         load_w(1)
+        load_x(1, 0, 1)
         load_w(2)
-        load_x(1, 0, 4)
+        load_x(1, 1, 4)
         nc.sync.dma_start(gates[1][:], gate[0:P, W:S])
 
         for m in range(BLOCKS - 1):
@@ -138,9 +140,24 @@ def tile_picked_place_lin_relu2_sub_l_kernel(tc, xT, w_words, w_scales, b, gate,
         for e0 in (0, H):
             interleave(0, 3, e0, e0 + H, 48)
             quantize(0, 3, e0, e0 + H)
+        rect_first = keep.tile([P, H], F32, name="rect_first", tag="late")
+        multiply(0, 0, 0, 0, H, rect_first[:])
+        twin = psum.tile([P, H], F32, name="acc5")
+        for a in range(PASSES):
+            nc.tensor.matmul_mx(
+                twin[:],
+                lhsT=w_codes[0][:, a, :].bitcast(FP8X4),
+                lhsT_scale=w_plane[4 * a : P, 0:P],
+                rhs=codes[0][:, a, 0:H].bitcast(FP8X4),
+                rhs_scale=plane[0][:, a, 0:H],
+                start=(a == 0),
+                stop=(a == PASSES - 1),
+            )
+        nc.vector.scalar_tensor_tensor(sqr[0][:, 0:H], twin[:], bias[:, 0:1], gates[0][:, 0:H], ADD, MULT)
+        nc.vector.tensor_tensor(windows[0][:].indirect(offsets[:, 0 : H // 16]), rect_first[:], sqr[0][:, 0:H], MULT)
         windows.append(keep.tile([P, T], F32, name="window3", tag="late"))
-        nc.vector.memset(windows[3][:], 0.0)
-        for bank, m, e0, e1 in ((0, 0, 0, H), (1, 0, H, W), (2, 1, 0, W), (3, 2, 0, W)):
+        nc.gpsimd.memset(windows[3][:], 0.0)
+        for bank, m, e0, e1 in ((1, 0, H, W), (2, 1, 0, W), (3, 2, 0, W)):
             cell(bank, 0, m, e0, e1)
         multiply(4, 0, 3, 0, W, rect_early[:, 3 * W : 4 * W])
         grouped.append(keep.tile([P, PASSES, W, PACK], BF16, align_bytes=64, name="grouped1"))

@@ -85,9 +85,8 @@ def tile_picked_place_lin_relu2_sub_l_kernel(tc, xT, w_words, w_scales, b, gate,
         nc.scalar.copy(bias[:], turned[:, 0:BLOCKS])
         nc.sync.dma_start(gates[0][:], gate[0:P, 0:W])
         load_w(1)
-        load_x(1, 0, 1)
         load_w(2)
-        load_x(1, 1, 4)
+        load_x(1, 0, 4)
         nc.sync.dma_start(gates[1][:], gate[0:P, W:S])
 
         for m in range(BLOCKS - 1):

@@ -48,13 +48,14 @@ def tile_picked_place_lin_relu2_sub_l_kernel(tc, xT, w_words, w_scales, b, gate,
         w_first = (0, 1, 2)
         w_codes = [keep.tile([P, PASSES, n * P], U32, align_bytes=64, name=f"w_codes{i}") for i, n in enumerate(w_sizes)]
         windows = [keep.tile([P, T], F32, name=f"window{m}") for m in range(BLOCKS - 1)]
-        raw = [
-            [keep.tile([P, PACK, W], F32, name=f"raw{c}_{a}", tag=f"raw{c}_{a}") for a in range(PASSES)]
-            for c in range(CHUNKS)
-        ]
+        raw = [[keep.tile([P, PACK, W], F32, name=f"raw{c}_{a}") for a in range(PASSES - 2 * c)] for c in range(CHUNKS)]
+        raw_half = [[keep.tile([P, PACK, H], F32, name=f"raw_half{h}_{a}") for a in range(2)] for h in range(2)]
+        grouped_half = [keep.tile([P, PASSES, H, PACK], BF16, align_bytes=64, name=f"grouped_half{h}") for h in range(2)]
+        codes_half = [keep.tile([P, PASSES, H], U32, align_bytes=64, name=f"codes_half{h}") for h in range(2)]
+        plane_half = [keep.tile([P, PASSES, H], U8, align_bytes=64, name=f"plane_half{h}") for h in range(2)]
         grouped = [keep.tile([P, PASSES, W, PACK], BF16, align_bytes=64, name="grouped0")]
-        codes = [keep.tile([P, PASSES, W], U32, align_bytes=64, name=f"codes{c}") for c in range(CHUNKS)]
-        plane = [keep.tile([P, PASSES, W], U8, align_bytes=64, name=f"plane{c}") for c in range(CHUNKS)]
+        codes = [keep.tile([P, PASSES, W], U32, align_bytes=64, name=f"codes{c}") for c in range(1)]
+        plane = [keep.tile([P, PASSES, W], U8, align_bytes=64, name=f"plane{c}") for c in range(1)]
         rect_early = keep.tile([P, BLOCKS * W], F32, align_bytes=64, name="rect_early")
         rect_late = keep.tile([P, BLOCKS * W], F32, name="rect_late")
         sqr = [keep.tile([P, BLOCKS * W], F32, name=f"sqr{c}") for c in range(CHUNKS)]
@@ -70,8 +71,8 @@ def tile_picked_place_lin_relu2_sub_l_kernel(tc, xT, w_words, w_scales, b, gate,
             nc.sync.dma_start(w_codes[i][:].bitcast(I32), w_rows[:, :, m0 * P * 4 : (m0 + n) * P * 4].bitcast(I32))
 
         nc.gpsimd.memset(w_plane[:].bitcast(U32), 0)
-        load_x(0, 0, 1)
         nc.sync.dma_start(offsets[:], offs)
+        load_x(0, 0, 1)
         load_x(0, 1, 2)
         for q in range(4):
             nc.sync.dma_start(w_plane[32 * q : 32 * q + 16, :].bitcast(I32), w_scales[:, 4 * q : 4 * q + 4, :].bitcast(I32))
@@ -86,7 +87,11 @@ def tile_picked_place_lin_relu2_sub_l_kernel(tc, xT, w_words, w_scales, b, gate,
         nc.sync.dma_start(gates[0][:], gate[0:P, 0:W])
         load_w(1)
         load_w(2)
-        load_x(1, 0, 4)
+        load_x(1, 0, 2)
+        for h in range(2):
+            for a in range(2, PASSES):
+                e0 = W + h * H
+                nc.sync.dma_start(raw_half[h][a - 2][:], xT[a * K_PASS : (a + 1) * K_PASS, e0 : e0 + H].rearrange("(p j) w -> p j w", j=PACK))
         nc.sync.dma_start(gates[1][:], gate[0:P, W:S])
 
         for m in range(BLOCKS - 1):
@@ -159,16 +164,48 @@ def tile_picked_place_lin_relu2_sub_l_kernel(tc, xT, w_words, w_scales, b, gate,
         for bank, m, e0, e1 in ((1, 0, H, W), (2, 1, 0, W), (3, 2, 0, W)):
             cell(bank, 0, m, e0, e1)
         multiply(4, 0, 3, 0, W, rect_early[:, 3 * W : 4 * W])
-        grouped.append(keep.tile([P, PASSES, W, PACK], BF16, align_bytes=64, name="grouped1"))
-        for a in range(PASSES):
-            interleave(1, a, 0, H, H)
-            interleave(1, a, H, W, H if a < 3 else 0)
-            quantize(1, a, 0, W)
-        put_back(0, 3, 0, W, rect_early[:, 3 * W : 4 * W], raw[1][3][:, 0, :])
-        multiply(0, 1, 0, 0, H, rect_late[:, 0:H])
-        multiply(1, 1, 0, H, W, rect_late[:, H:W])
-        put_back(1, 0, 0, W, rect_late[:, 0:W], sqr[1][:, 0:W])
-        nc.sync.dma_start(out[0:P, :], windows[0][:])
-        for m in range(1, BLOCKS):
-            cell((m - 1) % 2, 1, m, 0, W)
+
+        def interleave_half(h):
+            for a in range(PASSES):
+                source = raw[1][a][:, :, h * H : (h + 1) * H] if a < 2 else raw_half[h][a - 2][:]
+                nc.scalar.copy(
+                    grouped_half[h][:, a].rearrange("p (g i) j -> p g j i", i=RUN),
+                    source.rearrange("p j (g i) -> p g j i", i=RUN),
+                )
+            nc.vector.quantize_mx(
+                codes_half[h][:].rearrange("p a w -> p (a w)").bitcast(FP8X4),
+                plane_half[h][:].rearrange("p a w -> p (a w)"),
+                grouped_half[h][:].rearrange("p a w j -> p (a w j)"),
+            )
+
+        def multiply_half(h, m):
+            i = min(m, 2)
+            at = (m - w_first[i]) * P
+            acc = psum.tile([P, H], F32, name=f"acc{m % 2}")
+            for a in range(PASSES):
+                nc.tensor.matmul_mx(
+                    acc[:],
+                    lhsT=w_codes[i][:, a, at : at + P].bitcast(FP8X4),
+                    lhsT_scale=w_plane[4 * a : P, m * P : (m + 1) * P],
+                    rhs=codes_half[h][:, a, :].bitcast(FP8X4),
+                    rhs_scale=plane_half[h][:, a, :],
+                    start=(a == 0),
+                    stop=(a == PASSES - 1),
+                )
+            rect = rect_late[:, m * W + h * H : m * W + (h + 1) * H]
+            nc.scalar.activation(rect, acc[:], RELU, bias=bias[:, m : m + 1])
+            return rect
+
+        interleave_half(0)
+        put_back(0, 3, 0, W, rect_early[:, 3 * W : 4 * W], raw_half[0][1][:, 0:2, :].rearrange("p j w -> p (j w)"))
+        first = [multiply_half(0, m) for m in range(BLOCKS)]
+        put_back(1, 0, 0, H, first[0], sqr[1][:, 0:H])
+        interleave_half(1)
+        put_back(1, 1, 0, H, first[1], raw_half[1][1][:, 0, :])
+        put_back(1, 2, 0, H, first[2], raw_half[1][1][:, 1, :])
+        for m in range(BLOCKS - 1):
+            put_back(1, m, H, W, multiply_half(1, m), sqr[1][:, m * W + H : (m + 1) * W])
             nc.sync.dma_start(out[m * P : (m + 1) * P, :], windows[m][:])
+        multiply_half(1, 3)
+        put_back(1, 3, 0, W, rect_late[:, 3 * W : 4 * W], sqr[1][:, 3 * W : 4 * W])
+        nc.sync.dma_start(out[3 * P : 4 * P, :], windows[3][:])

@@ -10,6 +10,7 @@ K_PASS = P * PACK
 PASSES = K // K_PASS
 BLOCKS = N // P
 W = 256
+H = W // 2
 CHUNKS = S // W
 RUN = 2
 
@@ -35,8 +36,6 @@ def tile_picked_place_lin_relu2_sub_l_kernel(tc, xT, w_words, w_scales, b, gate,
     with ExitStack() as ctx:
         keep = ctx.enter_context(tc.tile_pool(name="keep", bufs=1))
         psum = ctx.enter_context(tc.psum_pool(name="psum", bufs=1))
-        psum_once = ctx.enter_context(tc.psum_pool(name="psum_once", bufs=1))
-        H = W // 2
 
         offsets = keep.tile([P, S // 16], U16, name="offsets")
         bias = keep.tile([P, BLOCKS], F32, name="bias")
@@ -45,167 +44,159 @@ def tile_picked_place_lin_relu2_sub_l_kernel(tc, xT, w_words, w_scales, b, gate,
         gates = [keep.tile([P, W], F32, name=f"gate{c}") for c in range(CHUNKS)]
         w_plane = keep.tile([P, N], U8, align_bytes=64, name="w_plane")
         w_sizes = (1, 1, 2)
-        w_first = (0, 1, 2)
         w_codes = [keep.tile([P, PASSES, n * P], U32, align_bytes=64, name=f"w_codes{i}") for i, n in enumerate(w_sizes)]
         windows = [keep.tile([P, T], F32, name=f"window{m}") for m in range(BLOCKS - 1)]
-        raw = [[keep.tile([P, PACK, W], F32, name=f"raw{c}_{a}") for a in range(PASSES - 2 * c)] for c in range(CHUNKS)]
-        raw_half = [[keep.tile([P, PACK, H], F32, name=f"raw_half{h}_{a}") for a in range(2)] for h in range(2)]
-        grouped_half = [keep.tile([P, PASSES, H, PACK], BF16, align_bytes=64, name=f"grouped_half{h}") for h in range(2)]
+        whole = (4, 2)
+        raw = {}
+        for c in range(CHUNKS):
+            for a in range(PASSES):
+                if a < whole[c]:
+                    raw[c, a] = keep.tile([P, PACK, W], F32, name=f"raw{c}_{a}")
+                else:
+                    for h in range(2):
+                        raw[c, a, h] = keep.tile([P, PACK, H], F32, name=f"raw{c}_{a}_{h}")
+        grouped = keep.tile([P, PASSES, W, PACK], BF16, align_bytes=64, name="grouped")
+        codes = keep.tile([P, PASSES, W], U32, align_bytes=64, name="codes")
+        plane = keep.tile([P, PASSES, W], U8, align_bytes=64, name="plane")
         codes_half = [keep.tile([P, PASSES, H], U32, align_bytes=64, name=f"codes_half{h}") for h in range(2)]
         plane_half = [keep.tile([P, PASSES, H], U8, align_bytes=64, name=f"plane_half{h}") for h in range(2)]
-        grouped = [keep.tile([P, PASSES, W, PACK], BF16, align_bytes=64, name="grouped0")]
-        codes = [keep.tile([P, PASSES, W], U32, align_bytes=64, name=f"codes{c}") for c in range(1)]
-        plane = [keep.tile([P, PASSES, W], U8, align_bytes=64, name=f"plane{c}") for c in range(1)]
-        rect_early = keep.tile([P, BLOCKS * W], F32, align_bytes=64, name="rect_early")
-        rect_late = keep.tile([P, BLOCKS * W], F32, name="rect_late")
+        rect = [keep.tile([P, BLOCKS * W], F32, name=f"rect{c}") for c in range(CHUNKS)]
         sqr = [keep.tile([P, BLOCKS * W], F32, name=f"sqr{c}") for c in range(CHUNKS)]
 
         w_rows = w_words.rearrange("a p m r -> p a (m r)")
 
-        def load_x(c, a0, a1):
-            for a in range(a0, a1):
-                nc.sync.dma_start(raw[c][a][:], xT[a * K_PASS : (a + 1) * K_PASS, c * W : (c + 1) * W].rearrange("(p j) w -> p j w", j=PACK))
+        def load_x(c, a, h=None):
+            e0, n, key = (c * W, W, (c, a)) if h is None else (c * W + h * H, H, (c, a, h))
+            nc.sync.dma_start(raw[key][:], xT[a * K_PASS : (a + 1) * K_PASS, e0 : e0 + n].rearrange("(p j) w -> p j w", j=PACK))
 
         def load_w(i):
-            m0, n = w_first[i], w_sizes[i]
-            nc.sync.dma_start(w_codes[i][:].bitcast(I32), w_rows[:, :, m0 * P * 4 : (m0 + n) * P * 4].bitcast(I32))
+            nc.sync.dma_start(w_codes[i][:].bitcast(I32), w_rows[:, :, i * P * 4 : (i + w_sizes[i]) * P * 4].bitcast(I32))
+
+        def load_scales(q):
+            nc.sync.dma_start(w_plane[32 * q : 32 * q + 16, :].bitcast(I32), w_scales[:, 4 * q : 4 * q + 4, :].bitcast(I32))
+
+        def load_gates(e0, e1):
+            nc.sync.dma_start(gates[e0 // W][:, e0 % W : e0 % W + e1 - e0], gate[0:P, e0:e1])
 
         nc.gpsimd.memset(w_plane[:].bitcast(U32), 0)
         nc.sync.dma_start(offsets[:], offs)
-        load_x(0, 0, 1)
-        load_x(0, 1, 2)
+        load_x(0, 0)
+        load_x(0, 1)
         for q in range(4):
-            nc.sync.dma_start(w_plane[32 * q : 32 * q + 16, :].bitcast(I32), w_scales[:, 4 * q : 4 * q + 4, :].bitcast(I32))
+            load_scales(q)
         nc.gpsimd.memset(bias_rows[:], 0.0)
         nc.gpsimd.dma_start(bias_rows[0:BLOCKS, :], b.rearrange("(m p) o -> m (p o)", p=P))
         load_w(0)
-        load_x(0, 2, 4)
-        make_identity(nc, identity[:])
-        turned = psum_once.tile([P, P], F32, name="turned")
-        nc.tensor.transpose(turned[:], bias_rows[:], identity[:])
-        nc.scalar.copy(bias[:], turned[:, 0:BLOCKS])
-        nc.sync.dma_start(gates[0][:], gate[0:P, 0:W])
+        load_x(0, 2)
+        load_x(0, 3)
+        load_gates(0, W)
         load_w(1)
         load_w(2)
-        load_x(1, 0, 2)
-        for h in range(2):
-            for a in range(2, PASSES):
-                e0 = W + h * H
-                nc.sync.dma_start(raw_half[h][a - 2][:], xT[a * K_PASS : (a + 1) * K_PASS, e0 : e0 + H].rearrange("(p j) w -> p j w", j=PACK))
-        nc.sync.dma_start(gates[1][:], gate[0:P, W:S])
+        load_x(1, 0)
+        load_x(1, 1)
+        load_x(1, 2, 0)
+        load_x(1, 3, 0)
+        load_x(1, 2, 1)
+        load_x(1, 3, 1)
+        load_gates(W, S)
+        make_identity(nc, identity[:])
+        turned = psum.tile([P, P], F32, name="turned")
+        nc.tensor.transpose(turned[:], bias_rows[:], identity[:])
+        nc.scalar.copy(bias[:], turned[:, 0:BLOCKS])
 
         for m in range(BLOCKS - 1):
             nc.vector.memset(windows[m][:], 0.0)
 
-        def interleave(c, a, e0, e1, share):
-            for engine_copy, w0, w1 in ((nc.scalar.copy, e0, e0 + share), (nc.vector.tensor_copy, e0 + share, e1)):
-                if w1 > w0:
-                    engine_copy(
-                        grouped[c][:, a, w0:w1].rearrange("p (g i) j -> p g j i", i=RUN),
-                        raw[c][a][:, :, w0:w1].rearrange("p j (g i) -> p g j i", i=RUN),
+        def source(c, a, e0, e1):
+            if a < whole[c]:
+                return raw[c, a][:, :, e0:e1]
+            return raw[c, a, e0 // H][:, :, e0 % H : e0 % H + e1 - e0]
+
+        def interleave(copy, target, c, a, e0, e1):
+            copy(target.rearrange("p (g i) j -> p g j i", i=RUN), source(c, a, e0, e1).rearrange("p j (g i) -> p g j i", i=RUN))
+
+        def quantize_early(a, e0, e1, share):
+            interleave(nc.scalar.copy, grouped[:, a, e0 : e0 + share], 0, a, e0, e0 + share)
+            interleave(nc.vector.tensor_copy, grouped[:, a, e0 + share : e1], 0, a, e0 + share, e1)
+            nc.vector.quantize_mx(codes[:, a, e0:e1].bitcast(FP8X4), plane[:, a, e0:e1], grouped[:, a, e0:e1].rearrange("p w j -> p (w j)"))
+
+        staged = keep.tile([P, 2 * PASSES * H * PACK], BF16, align_bytes=64, name="staged")
+        by_pass = staged[:].rearrange("p (h a w j) -> p a h w j", h=2, a=PASSES, j=PACK)
+
+        def quantize_late(h):
+            for a in range(PASSES):
+                if a >= whole[1]:
+                    interleave(nc.scalar.copy, by_pass[:, a, h], 1, a, h * H, (h + 1) * H)
+                elif h == 0:
+                    nc.scalar.copy(
+                        by_pass[:, a].rearrange("p h (g i) j -> p h g j i", i=RUN),
+                        raw[1, a][:].rearrange("p j (h g i) -> p h g j i", h=2, i=RUN),
                     )
-
-        def quantize(c, a, e0, e1):
-            nc.vector.quantize_mx(
-                codes[c][:, a, e0:e1].bitcast(FP8X4),
-                plane[c][:, a, e0:e1],
-                grouped[c][:, a, e0:e1].rearrange("p w j -> p (w j)"),
-            )
-
-        def multiply(bank, c, m, e0, e1, rect):
-            i = min(m, 2)
-            at = (m - w_first[i]) * P
-            acc = psum.tile([P, e1 - e0], F32, name=f"acc{bank}")
-            for a in range(PASSES):
-                nc.tensor.matmul_mx(
-                    acc[:],
-                    lhsT=w_codes[i][:, a, at : at + P].bitcast(FP8X4),
-                    lhsT_scale=w_plane[4 * a : P, m * P : (m + 1) * P],
-                    rhs=codes[c][:, a, e0:e1].bitcast(FP8X4),
-                    rhs_scale=plane[c][:, a, e0:e1],
-                    start=(a == 0),
-                    stop=(a == PASSES - 1),
-                )
-            nc.scalar.activation(rect, acc[:], RELU, bias=bias[:, m : m + 1])
-
-        def put_back(c, m, e0, e1, rect, squares):
-            nc.scalar.activation(squares, rect, SQUARE)
-            listed = offsets[:, (c * W + e0) // 16 : (c * W + e1) // 16]
-            nc.vector.tensor_tensor(windows[m][:].indirect(listed), squares, gates[c][:, e0:e1], MULT)
-
-        def cell(bank, c, m, e0, e1):
-            rect = (rect_early, rect_late)[c][:, m * W + e0 : m * W + e1]
-            multiply(bank, c, m, e0, e1, rect)
-            put_back(c, m, e0, e1, rect, sqr[c][:, m * W + e0 : m * W + e1])
-
-        for a in range(PASSES - 1):
-            interleave(0, a, 0, W, 96)
-            quantize(0, a, 0, W)
-        for e0 in (0, H):
-            interleave(0, 3, e0, e0 + H, 48)
-            quantize(0, 3, e0, e0 + H)
-        rect_first = keep.tile([P, H], F32, name="rect_first", tag="late")
-        multiply(0, 0, 0, 0, H, rect_first[:])
-        twin = psum.tile([P, H], F32, name="acc5")
-        for a in range(PASSES):
-            nc.tensor.matmul_mx(
-                twin[:],
-                lhsT=w_codes[0][:, a, :].bitcast(FP8X4),
-                lhsT_scale=w_plane[4 * a : P, 0:P],
-                rhs=codes[0][:, a, 0:H].bitcast(FP8X4),
-                rhs_scale=plane[0][:, a, 0:H],
-                start=(a == 0),
-                stop=(a == PASSES - 1),
-            )
-        nc.vector.scalar_tensor_tensor(sqr[0][:, 0:H], twin[:], bias[:, 0:1], gates[0][:, 0:H], ADD, MULT)
-        nc.vector.tensor_tensor(windows[0][:].indirect(offsets[:, 0 : H // 16]), rect_first[:], sqr[0][:, 0:H], MULT)
-        windows.append(keep.tile([P, T], F32, name="window3", tag="late"))
-        nc.gpsimd.memset(windows[3][:], 0.0)
-        for bank, m, e0, e1 in ((1, 0, H, W), (2, 1, 0, W), (3, 2, 0, W)):
-            cell(bank, 0, m, e0, e1)
-        multiply(4, 0, 3, 0, W, rect_early[:, 3 * W : 4 * W])
-
-        def interleave_half(h):
-            for a in range(PASSES):
-                source = raw[1][a][:, :, h * H : (h + 1) * H] if a < 2 else raw_half[h][a - 2][:]
-                nc.scalar.copy(
-                    grouped_half[h][:, a].rearrange("p (g i) j -> p g j i", i=RUN),
-                    source.rearrange("p j (g i) -> p g j i", i=RUN),
-                )
             nc.vector.quantize_mx(
                 codes_half[h][:].rearrange("p a w -> p (a w)").bitcast(FP8X4),
                 plane_half[h][:].rearrange("p a w -> p (a w)"),
-                grouped_half[h][:].rearrange("p a w j -> p (a w j)"),
+                staged[:, h * PASSES * H * PACK : (h + 1) * PASSES * H * PACK],
             )
 
-        def multiply_half(h, m):
+        def sums(bank, c, m, e0, e1, last_first=False):
             i = min(m, 2)
-            at = (m - w_first[i]) * P
-            acc = psum.tile([P, H], F32, name=f"acc{m % 2}")
-            for a in range(PASSES):
+            at = (m - i) * P
+            acc = psum.tile([P, e1 - e0], F32, name=f"acc{bank}")
+            order = range(PASSES - 1, -1, -1) if last_first else range(PASSES)
+            for a in order:
                 nc.tensor.matmul_mx(
                     acc[:],
                     lhsT=w_codes[i][:, a, at : at + P].bitcast(FP8X4),
                     lhsT_scale=w_plane[4 * a : P, m * P : (m + 1) * P],
-                    rhs=codes_half[h][:, a, :].bitcast(FP8X4),
-                    rhs_scale=plane_half[h][:, a, :],
-                    start=(a == 0),
-                    stop=(a == PASSES - 1),
+                    rhs=(codes[:, a, e0:e1] if c == 0 else codes_half[e0 // H][:, a, :]).bitcast(FP8X4),
+                    rhs_scale=plane[:, a, e0:e1] if c == 0 else plane_half[e0 // H][:, a, :],
+                    start=(a == order[0]),
+                    stop=(a == order[-1]),
                 )
-            rect = rect_late[:, m * W + h * H : m * W + (h + 1) * H]
-            nc.scalar.activation(rect, acc[:], RELU, bias=bias[:, m : m + 1])
-            return rect
+            return acc
 
-        interleave_half(0)
-        put_back(0, 3, 0, W, rect_early[:, 3 * W : 4 * W], raw_half[0][1][:, 0:2, :].rearrange("p j w -> p (j w)"))
-        first = [multiply_half(0, m) for m in range(BLOCKS)]
-        put_back(1, 0, 0, H, first[0], sqr[1][:, 0:H])
-        interleave_half(1)
-        put_back(1, 1, 0, H, first[1], raw_half[1][1][:, 0, :])
-        put_back(1, 2, 0, H, first[2], raw_half[1][1][:, 1, :])
-        for m in range(BLOCKS - 1):
-            put_back(1, m, H, W, multiply_half(1, m), sqr[1][:, m * W + H : (m + 1) * W])
+        def rectify(bank, c, m, e0, e1, target=None, last_first=False):
+            if target is None:
+                target = rect[c][:, m * W + e0 : m * W + e1]
+            nc.scalar.activation(target, sums(bank, c, m, e0, e1, last_first)[:], RELU, bias=bias[:, m : m + 1])
+            return target
+
+        def scatter(c, m, e0, e1, in0, in1):
+            nc.vector.tensor_tensor(windows[m][:].indirect(offsets[:, (c * W + e0) // 16 : (c * W + e1) // 16]), in0, in1, MULT)
+
+        def put_back(c, m, e0, e1, rectified, squares=None):
+            if squares is None:
+                squares = sqr[c][:, m * W + e0 : m * W + e1]
+            nc.scalar.activation(squares, rectified, SQUARE)
+            scatter(c, m, e0, e1, squares, gates[c][:, e0:e1])
+
+        def store(m):
             nc.sync.dma_start(out[m * P : (m + 1) * P, :], windows[m][:])
-        multiply_half(1, 3)
-        put_back(1, 3, 0, W, rect_late[:, 3 * W : 4 * W], sqr[1][:, 3 * W : 4 * W])
-        nc.sync.dma_start(out[3 * P : 4 * P, :], windows[3][:])
+
+        for a in range(3):
+            quantize_early(a, 0, W, 96)
+        for e0 in (0, H):
+            quantize_early(3, e0, e0 + H, 48)
+        rect_first = keep.tile([P, H], F32, name="rect_first", tag="late")
+        rectify(0, 0, 0, 0, H, rect_first[:])
+        nc.vector.scalar_tensor_tensor(sqr[0][:, 0:H], sums(5, 0, 0, 0, H)[:], bias[:, 0:1], gates[0][:, 0:H], ADD, MULT)
+        scatter(0, 0, 0, H, rect_first[:], sqr[0][:, 0:H])
+        windows.append(keep.tile([P, T], F32, name="window3", tag="late"))
+        nc.gpsimd.memset(windows[3][:], 0.0)
+        put_back(0, 0, H, W, rectify(1, 0, 0, H, W))
+        put_back(0, 1, 0, W, rectify(2, 0, 1, 0, W))
+        put_back(0, 2, 0, W, rectify(3, 0, 2, 0, W))
+        held = rectify(4, 0, 3, 0, W)
+        quantize_late(0)
+        put_back(0, 3, 0, W, held, raw[1, 2, 0][:, 0:2, :].rearrange("p j w -> p (j w)"))
+        quantize_late(1)
+        for m in range(2):
+            put_back(1, m, 0, H, rectify(m, 1, m, 0, H, raw[1, 3, 1][:, m, :]))
+        for m in range(2):
+            put_back(1, m, H, W, rectify(m, 1, m, H, W))
+            store(m)
+        for m in range(2, BLOCKS):
+            for h in range(2):
+                rectify(h, 1, m, h * H, (h + 1) * H)
+            put_back(1, m, 0, W, rect[1][:, m * W : (m + 1) * W])
+            store(m)

@@ -120,22 +120,14 @@ def tile_picked_place_lin_relu2_sub_l_kernel(tc, xT, w_words, w_scales, b, gate,
             interleave(nc.vector.tensor_copy, grouped[:, a, e0 + share : e1], 0, a, e0 + share, e1)
             nc.vector.quantize_mx(codes[:, a, e0:e1].bitcast(FP8X4), plane[:, a, e0:e1], grouped[:, a, e0:e1].rearrange("p w j -> p (w j)"))
 
-        staged = keep.tile([P, 2 * PASSES * H * PACK], BF16, align_bytes=64, name="staged")
-        by_pass = staged[:].rearrange("p (h a w j) -> p a h w j", h=2, a=PASSES, j=PACK)
-
-        def quantize_late(h):
+        def quantize_late(h, tag):
+            staged = keep.tile([P, PASSES, H, PACK], BF16, align_bytes=64, name=f"staged{h}", tag=tag)
             for a in range(PASSES):
-                if a >= whole[1]:
-                    interleave(nc.scalar.copy, by_pass[:, a, h], 1, a, h * H, (h + 1) * H)
-                elif h == 0:
-                    nc.scalar.copy(
-                        by_pass[:, a].rearrange("p h (g i) j -> p h g j i", i=RUN),
-                        raw[1, a][:].rearrange("p j (h g i) -> p h g j i", h=2, i=RUN),
-                    )
+                interleave(nc.vector.tensor_copy if (h, a) == (1, 3) else nc.scalar.copy, staged[:, a], 1, a, h * H, (h + 1) * H)
             nc.vector.quantize_mx(
                 codes_half[h][:].rearrange("p a w -> p (a w)").bitcast(FP8X4),
                 plane_half[h][:].rearrange("p a w -> p (a w)"),
-                staged[:, h * PASSES * H * PACK : (h + 1) * PASSES * H * PACK],
+                staged[:].rearrange("p a w j -> p (a w j)"),
             )
 
         def sums(bank, c, m, e0, e1, last_first=False):
@@ -187,11 +179,11 @@ def tile_picked_place_lin_relu2_sub_l_kernel(tc, xT, w_words, w_scales, b, gate,
         put_back(0, 1, 0, W, rectify(2, 0, 1, 0, W))
         put_back(0, 2, 0, W, rectify(3, 0, 2, 0, W))
         held = rectify(4, 0, 3, 0, W)
-        quantize_late(0)
-        put_back(0, 3, 0, W, held, raw[1, 2, 0][:, 0:2, :].rearrange("p j w -> p (j w)"))
-        quantize_late(1)
+        quantize_late(0, "staged0")
+        put_back(0, 3, 0, W, held, raw[1, 3, 0][:, 0:2, :].rearrange("p j w -> p (j w)"))
+        quantize_late(1, "staged1")
         for m in range(2):
-            put_back(1, m, 0, H, rectify(m, 1, m, 0, H, raw[1, 3, 1][:, m, :]))
+            put_back(1, m, 0, H, rectify(m, 1, m, 0, H, raw[1, 2, 1][:, m, :]))
         for m in range(2):
             put_back(1, m, H, W, rectify(m, 1, m, H, W))
             store(m)

from contextlib import ExitStack

import concourse.mybir as mybir
from concourse.masks import make_identity

K, T, S, N = 2048, 1024, 512, 512
P = 128
PACK = 4
K_PASS = P * PACK
PASSES = K // K_PASS
BLOCKS = N // P
W = 256
H = W // 2
CHUNKS = S // W
RUN = 2

F32 = mybir.dt.float32
BF16 = mybir.dt.bfloat16
I32 = mybir.dt.int32
U32 = mybir.dt.uint32
U16 = mybir.dt.uint16
U8 = mybir.dt.uint8
FP8X4 = mybir.dt.float8_e4m3fn_x4

RELU = mybir.ActivationFunctionType.Relu
SQUARE = mybir.ActivationFunctionType.Square
MULT = mybir.AluOpType.mult
ADD = mybir.AluOpType.add

FLOPS = 2 * K * S * N
BYTES = 4 * K * S + K * N + K * N // 32 + 4 * N + 4 * S + 16 * S + 4 * N * T


def tile_picked_place_lin_relu2_sub_l_kernel(tc, xT, w_words, w_scales, b, gate, offs, out):
    nc = tc.nc
    with ExitStack() as ctx:
        keep = ctx.enter_context(tc.tile_pool(name="keep", bufs=1))
        psum = ctx.enter_context(tc.psum_pool(name="psum", bufs=1))

        offsets = keep.tile([P, S // 16], U16, name="offsets")
        bias = keep.tile([P, BLOCKS], F32, name="bias")
        bias_rows = keep.tile([P, P], F32, name="bias_rows")
        identity = keep.tile([P, P], F32, name="identity")
        gates = [keep.tile([P, W], F32, name=f"gate{c}") for c in range(CHUNKS)]
        w_plane = keep.tile([P, N], U8, align_bytes=64, name="w_plane")
        w_sizes = (1, 1, 2)
        w_codes = [keep.tile([P, PASSES, n * P], U32, align_bytes=64, name=f"w_codes{i}") for i, n in enumerate(w_sizes)]
        windows = [keep.tile([P, T], F32, name=f"window{m}") for m in range(BLOCKS - 1)]
        whole = (4, 2)
        raw = {}
        for c in range(CHUNKS):
            for a in range(PASSES):
                if a < whole[c]:
                    raw[c, a] = keep.tile([P, PACK, W], F32, name=f"raw{c}_{a}")
                else:
                    for h in range(2):
                        raw[c, a, h] = keep.tile([P, PACK, H], F32, name=f"raw{c}_{a}_{h}")
        grouped = keep.tile([P, PASSES, W, PACK], BF16, align_bytes=64, name="grouped")
        codes = keep.tile([P, PASSES, W], U32, align_bytes=64, name="codes")
        plane = keep.tile([P, PASSES, W], U8, align_bytes=64, name="plane")
        codes_half = [keep.tile([P, PASSES, H], U32, align_bytes=64, name=f"codes_half{h}") for h in range(2)]
        plane_half = [keep.tile([P, PASSES, H], U8, align_bytes=64, name=f"plane_half{h}") for h in range(2)]
        rect = [keep.tile([P, BLOCKS * W], F32, name=f"rect{c}") for c in range(CHUNKS)]
        sqr = [keep.tile([P, BLOCKS * W], F32, name=f"sqr{c}") for c in range(CHUNKS)]

        w_rows = w_words.rearrange("a p m r -> p a (m r)")

        def load_x(c, a, h=None):
            e0, n, key = (c * W, W, (c, a)) if h is None else (c * W + h * H, H, (c, a, h))
            nc.sync.dma_start(raw[key][:], xT[a * K_PASS : (a + 1) * K_PASS, e0 : e0 + n].rearrange("(p j) w -> p j w", j=PACK))

        def load_w(i):
            nc.sync.dma_start(w_codes[i][:].bitcast(I32), w_rows[:, :, i * P * 4 : (i + w_sizes[i]) * P * 4].bitcast(I32))

        def load_scales(q):
            nc.sync.dma_start(w_plane[32 * q : 32 * q + 16, :].bitcast(I32), w_scales[:, 4 * q : 4 * q + 4, :].bitcast(I32))

        def load_gates(e0, e1):
            nc.sync.dma_start(gates[e0 // W][:, e0 % W : e0 % W + e1 - e0], gate[0:P, e0:e1])

        nc.gpsimd.memset(w_plane[:].bitcast(U32), 0)
        nc.sync.dma_start(offsets[:], offs)
        load_x(0, 0)
        load_x(0, 1)
        for q in range(4):
            load_scales(q)
        nc.gpsimd.memset(bias_rows[:], 0.0)
        nc.gpsimd.dma_start(bias_rows[0:BLOCKS, :], b.rearrange("(m p) o -> m (p o)", p=P))
        load_w(0)
        load_x(0, 2)
        load_x(0, 3)
        load_gates(0, W)
        load_w(1)
        load_w(2)
        load_x(1, 0)
        load_x(1, 1)
        load_x(1, 2, 0)
        load_x(1, 3, 0)
        load_x(1, 2, 1)
        load_x(1, 3, 1)
        load_gates(W, S)
        make_identity(nc, identity[:])
        turned = psum.tile([P, P], F32, name="turned")
        nc.tensor.transpose(turned[:], bias_rows[:], identity[:])
        nc.scalar.copy(bias[:], turned[:, 0:BLOCKS])

        for m in range(BLOCKS - 1):
            nc.vector.memset(windows[m][:], 0.0)

        def source(c, a, e0, e1):
            if a < whole[c]:
                return raw[c, a][:, :, e0:e1]
            return raw[c, a, e0 // H][:, :, e0 % H : e0 % H + e1 - e0]

        def interleave(copy, target, c, a, e0, e1):
            copy(target.rearrange("p (g i) j -> p g j i", i=RUN), source(c, a, e0, e1).rearrange("p j (g i) -> p g j i", i=RUN))

        def quantize_early(a, e0, e1, share):
            interleave(nc.scalar.copy, grouped[:, a, e0 : e0 + share], 0, a, e0, e0 + share)
            interleave(nc.vector.tensor_copy, grouped[:, a, e0 + share : e1], 0, a, e0 + share, e1)
            nc.vector.quantize_mx(codes[:, a, e0:e1].bitcast(FP8X4), plane[:, a, e0:e1], grouped[:, a, e0:e1].rearrange("p w j -> p (w j)"))

        def quantize_late(h, tag):
            staged = keep.tile([P, PASSES, H, PACK], BF16, align_bytes=64, name=f"staged{h}", tag=tag)
            for a in range(PASSES):
                interleave(nc.vector.tensor_copy if (h, a) == (1, 3) else nc.scalar.copy, staged[:, a], 1, a, h * H, (h + 1) * H)
            nc.vector.quantize_mx(
                codes_half[h][:].rearrange("p a w -> p (a w)").bitcast(FP8X4),
                plane_half[h][:].rearrange("p a w -> p (a w)"),
                staged[:].rearrange("p a w j -> p (a w j)"),
            )

        def sums(bank, c, m, e0, e1, last_first=False):
            i = min(m, 2)
            at = (m - i) * P
            acc = psum.tile([P, e1 - e0], F32, name=f"acc{bank}")
            order = range(PASSES - 1, -1, -1) if last_first else range(PASSES)
            for a in order:
                nc.tensor.matmul_mx(
                    acc[:],
                    lhsT=w_codes[i][:, a, at : at + P].bitcast(FP8X4),
                    lhsT_scale=w_plane[4 * a : P, m * P : (m + 1) * P],
                    rhs=(codes[:, a, e0:e1] if c == 0 else codes_half[e0 // H][:, a, :]).bitcast(FP8X4),
                    rhs_scale=plane[:, a, e0:e1] if c == 0 else plane_half[e0 // H][:, a, :],
                    start=(a == order[0]),
                    stop=(a == order[-1]),
                )
            return acc

        def rectify(bank, c, m, e0, e1, target=None, last_first=False):
            if target is None:
                target = rect[c][:, m * W + e0 : m * W + e1]
            nc.scalar.activation(target, sums(bank, c, m, e0, e1, last_first)[:], RELU, bias=bias[:, m : m + 1])
            return target

        def scatter(c, m, e0, e1, in0, in1):
            nc.vector.tensor_tensor(windows[m][:].indirect(offsets[:, (c * W + e0) // 16 : (c * W + e1) // 16]), in0, in1, MULT)

        def put_back(c, m, e0, e1, rectified, squares=None):
            if squares is None:
                squares = sqr[c][:, m * W + e0 : m * W + e1]
            nc.scalar.activation(squares, rectified, SQUARE)
            scatter(c, m, e0, e1, squares, gates[c][:, e0:e1])

        def store(m):
            nc.sync.dma_start(out[m * P : (m + 1) * P, :], windows[m][:])

        for a in range(3):
            quantize_early(a, 0, W, 96)
        for e0 in (0, H):
            quantize_early(3, e0, e0 + H, 48)
        rect_first = keep.tile([P, H], F32, name="rect_first", tag="late")
        rectify(0, 0, 0, 0, H, rect_first[:])
        nc.vector.scalar_tensor_tensor(sqr[0][:, 0:H], sums(5, 0, 0, 0, H)[:], bias[:, 0:1], gates[0][:, 0:H], ADD, MULT)
        scatter(0, 0, 0, H, rect_first[:], sqr[0][:, 0:H])
        windows.append(keep.tile([P, T], F32, name="window3", tag="late"))
        nc.gpsimd.memset(windows[3][:], 0.0)
        put_back(0, 0, H, W, rectify(1, 0, 0, H, W))
        put_back(0, 1, 0, W, rectify(2, 0, 1, 0, W))
        put_back(0, 2, 0, W, rectify(3, 0, 2, 0, W))
        held = rectify(4, 0, 3, 0, W)
        quantize_late(0, "staged0")
        put_back(0, 3, 0, W, held, raw[1, 3, 0][:, 0:2, :].rearrange("p j w -> p (j w)"))
        quantize_late(1, "staged1")
        for m in range(2):
            put_back(1, m, 0, H, rectify(m, 1, m, 0, H, raw[1, 2, 1][:, m, :]))
        for m in range(2):
            put_back(1, m, H, W, rectify(m, 1, m, H, W))
            store(m)
        for m in range(2, BLOCKS):
            for h in range(2):
                rectify(h, 1, m, h * H, (h + 1) * H)
            put_back(1, m, 0, W, rect[1][:, m * W : (m + 1) * W])
            store(m)
